import numpy as np
import ml_dtypes


def mxq(x, axis, fmt="e4m3"):
    dtype, down = {"e4m3": (ml_dtypes.float8_e4m3fn, 7), "e5m2": (ml_dtypes.float8_e5m2, 14)}[fmt]
    v = np.moveaxis(np.asarray(x, np.float32).astype(ml_dtypes.bfloat16).astype(np.float64), axis, -1)
    blocks = v.reshape(v.shape[:-1] + (-1, 32))
    amax = np.abs(blocks).max(-1, keepdims=True)
    byte = np.maximum(np.where(amax > 0, np.frexp(amax)[1] - 1 + 127, 0) - down, 1)
    scale = np.exp2(byte - 127.0)
    codes = (blocks / scale).astype(np.float32).astype(dtype).astype(np.float64)
    return np.moveaxis((codes * scale).reshape(v.shape), -1, axis)


WIDE = False


def mx_kscale(k):
    if not WIDE:
        return np.ones(k)
    levels = np.array([10, -10, 5, -5, 0])
    if k % 512:
        return np.exp2(np.random.permutation(np.resize(levels, k // 32))).repeat(32)
    a = np.empty((k // 512, 16))
    for p in range(k // 512):
        a[p, :8] = np.random.permutation(np.resize(levels, 8))
        for g in range(8):
            far = levels[np.abs(levels - a[p, g]) >= 10]
            a[p, g + 8] = far[np.random.randint(len(far))]
    return np.exp2(a.ravel()).repeat(32)


def f64(x):
    return np.asarray(x).astype(np.float64)


def striped(idx):
    return np.tile(np.asarray(idx).reshape(-1, 16).T, (8, 1)).astype(np.uint16)


def unstriped(offs):
    return offs[:16].T.reshape(-1).astype(np.int64)


E2M1 = np.array([0.0, 0.5, 1.0, 1.5, 2.0, 3.0, 4.0, 6.0, -0.0, -0.5, -1.0, -1.5, -2.0, -3.0, -4.0, -6.0])


def pack_weight(w, fmt):
    k, n = w.shape
    w = f64(np.asarray(w, np.float32).astype(ml_dtypes.bfloat16)).reshape(k // 32, 32, n)
    amax = np.abs(w).max(1)
    if fmt == "e4m3":
        byte = np.frexp(amax)[1] - 1 + 127 - 7
    else:
        mant, ex = np.frexp(amax / 6.0)
        byte = np.where(mant > 0.5, ex, ex - 1) + 127
    byte = np.clip(np.where(amax > 0, byte, 1), 1, 254)
    scaled = (w * np.exp2(127.0 - byte)[:, None, :]).reshape(k, n).astype(np.float32)
    by_word = np.ascontiguousarray(scaled.reshape(k // 512, 128, 4, n).transpose(0, 1, 3, 2))
    if fmt == "e4m3":
        words = by_word.astype(ml_dtypes.float8_e4m3fn).view(np.uint8)
    else:
        c = by_word.astype(ml_dtypes.float4_e2m1fn).view(np.uint8) & 0xF
        words = (c[..., 0::2] | (c[..., 1::2] << 4)).reshape(k // 512, 128, 2 * n)
    return np.ascontiguousarray(words), np.ascontiguousarray(byte.astype(np.uint8).reshape(k // 512, 16, n))


def unpack_weight(words, scales, fmt):
    g, _, n = scales.shape
    words = np.ascontiguousarray(words).reshape(g, 128, n, -1)
    if fmt == "e4m3":
        vals = words.view(ml_dtypes.float8_e4m3fn).astype(np.float64)
    else:
        nib = np.empty((g, 128, n, 4), np.uint8)
        nib[..., 0::2] = words & 0xF
        nib[..., 1::2] = words >> 4
        vals = E2M1[nib]
    vals = vals * np.repeat(np.exp2(scales.astype(np.float64) - 127.0), 8, axis=1)[..., None]
    return vals.transpose(0, 1, 3, 2).reshape(g * 512, n)


D, T, I, Q, E = 512, 2048, 512, 128, 512


def setup_inputs():
    n = np.random.standard_normal
    idx = np.random.permutation(T)[:I]
    fd = mx_kscale(D)
    fi = mx_kscale(I)
    ti = np.ones(T)
    ti[idx] = fi
    keysp = pack_weight(n((D, T)) / fd[:, None], "e4m3")
    return {
        "query": (n((D, Q)) * 1.0 / np.sqrt(D) * fd[:, None]).astype(np.float32),
        "keys_words": keysp[0],
        "keys_scales": keysp[1],
        "steep": (np.random.uniform(0.7, 2.0, (Q, 1))).astype(np.float32),
        "base0": (np.random.uniform(-0.5, 0.5, (Q, 1))).astype(np.float32),
        "size": (np.random.uniform(2.0, 8.0, (1, I)) * fi).astype(np.float32),
        "vals": (n((E, T)) / ti).astype(np.float32),
        "offs": striped(idx),
    }


def reference(query, keys_words, keys_scales, steep, base0, size, vals, offs):
    idx = unstriped(offs)
    keysu = unpack_weight(keys_words, keys_scales, "e4m3")
    queryq = mxq(f64(query), 0, "e4m3")
    keysidxg = keysu[:, idx]
    a = queryq.T @ keysidxg
    p = np.tanh(a * f64(steep)) - f64(base0)
    w = p * f64(size) / np.sum(np.abs(p), axis=1, keepdims=True)
    wt = w.T
    vt = f64(vals)[:, idx].T
    wtq = mxq(wt, 0, "e4m3")
    vtq = mxq(vt, 0, "e4m3")
    o = wtq.T @ vtq
    return o

@@ -1,0 +1,139 @@
+from contextlib import ExitStack
+
+import concourse.mybir as mybir
+from concourse.masks import make_identity
+
+D, T, I, Q, E = 512, 2048, 512, 128, 512
+FLOPS = 2 * Q * D * I + 2 * Q * I * E
+
+F32 = mybir.dt.float32
+BF16 = mybir.dt.bfloat16
+I32 = mybir.dt.int32
+U32 = mybir.dt.uint32
+U16 = mybir.dt.uint16
+U8 = mybir.dt.uint8
+FP8X4 = mybir.dt.float8_e4m3fn_x4
+ACT = mybir.ActivationFunctionType
+ALU = mybir.AluOpType
+
+P = 128
+PACK = 4
+BLOCKS = E // P
+
+
+def tile_attend_signedread_kernel(tc, query, keys_words, keys_scales, steep, base0, size, vals, offs, out):
+    nc = tc.nc
+    with ExitStack() as ctx:
+        sb = ctx.enter_context(tc.tile_pool(name="sb", bufs=1))
+        ps = ctx.enter_context(tc.psum_pool(name="ps", bufs=1))
+
+        offsets = sb.tile([P, I // 16], U16, name="offsets")
+        nc.sync.dma_start(offsets[:], offs)
+
+        key_bytes = sb.tile([P, T], U8, name="key_bytes", align_bytes=64)
+        nc.vector.memset(key_bytes[:].bitcast(I32), 0)
+        for quad in range(4):
+            nc.scalar.dma_start(
+                key_bytes[32 * quad : 32 * quad + 4, :].bitcast(I32),
+                keys_scales[0, 4 * quad : 4 * quad + 4, :].bitcast(I32),
+            )
+
+        q_raw = sb.tile([P, PACK, Q], F32, name="q_raw")
+        nc.sync.dma_start(q_raw[:], query.rearrange("(p j) q -> p j q", j=PACK))
+        key_words = sb.tile([P, T], U32, name="key_words", align_bytes=64)
+        nc.sync.dma_start(key_words[:].bitcast(I32), keys_words[0].rearrange("p n t -> p (n t)").bitcast(I32))
+        pools = []
+        for b in range(BLOCKS):
+            pool_b = sb.tile([P, T], F32, name="val_pool%d" % b, align_bytes=64)
+            nc.sync.dma_start(pool_b[:], vals[b * P : (b + 1) * P, :])
+            pools.append(pool_b)
+
+        steep_col = sb.tile([P, 1], F32, name="steep_col")
+        nc.gpsimd.dma_start(steep_col[:], steep)
+        base_col = sb.tile([P, 1], F32, name="base_col")
+        nc.gpsimd.dma_start(base_col[:], base0)
+        size_cols = sb.tile([P, PACK], F32, name="size_cols")
+        nc.gpsimd.dma_start(size_cols[:], size.rearrange("o (p t) -> (o p) t", t=PACK))
+        ident = sb.tile([P, P], F32, name="ident")
+        make_identity(nc, ident[:])
+
+        def quantize(name, grouped, width):
+            codes = sb.tile([P, width], U32, name=name + "_codes", align_bytes=64)
+            plane = sb.tile([P, width], U8, name=name + "_plane", align_bytes=64)
+            nc.vector.quantize_mx(out=codes[:].bitcast(FP8X4), scales=plane[:], in_=grouped)
+            return codes, plane
+
+        q_grouped = sb.tile([P, Q, PACK], BF16, name="q_grouped", align_bytes=64)
+        nc.vector.tensor_copy(out=q_grouped[:], in_=q_raw[:].rearrange("p j q -> p q j"))
+        listed_bytes = sb.tile([P, I], U8, name="listed_bytes", align_bytes=64)
+        nc.vector.tensor_copy(listed_bytes[:], key_bytes[:].indirect(offsets[:]))
+        q_codes, q_plane = quantize("q", q_grouped[:].rearrange("p q j -> p (q j)"), Q)
+        listed_words = sb.tile([P, I], U32, name="listed_words", align_bytes=64)
+        nc.vector.tensor_copy(listed_words[:], key_words[:].indirect(offsets[:]))
+        scores = ps.tile([P, I], F32, name="scores")
+        nc.tensor.matmul_mx(
+            out=scores[:],
+            lhsT=q_codes[:].bitcast(FP8X4),
+            lhsT_scale=q_plane[:],
+            rhs=listed_words[:].bitcast(FP8X4),
+            rhs_scale=listed_bytes[:],
+            start=True,
+            stop=True,
+        )
+
+        tanhs = sb.tile([P, PACK, P], F32, name="tanhs")
+        nc.scalar.activation(
+            out=tanhs[:], in_=scores[:].rearrange("q (s t) -> q t s", t=PACK), func=ACT.Tanh, scale=steep_col[:]
+        )
+        magnitudes = sb.tile([P, PACK, P], F32, name="magnitudes")
+        row_sum = sb.tile([P, 1], F32, name="row_sum")
+        nc.scalar.activation(
+            out=magnitudes[:], in_=tanhs[:], func=ACT.Abs, scale=-1.0, bias=base_col[:], accum_out=row_sum[:]
+        )
+        row_inv = sb.tile([P, 1], F32, name="row_inv")
+        nc.vector.reciprocal(row_inv[:], row_sum[:])
+        normed = sb.tile([P, PACK, P], F32, name="normed")
+        nc.vector.tensor_scalar(normed[:], tanhs[:], base_col[:], row_inv[:], ALU.subtract, ALU.mult)
+        turned_w = ps.tile([P, PACK, Q], F32, name="turned_w")
+        for t in range(PACK):
+            nc.tensor.transpose(turned_w[:, t, :], normed[:, t, :], ident[:])
+        w_grouped = sb.tile([P, Q, PACK], BF16, name="w_grouped", align_bytes=64)
+        nc.vector.tensor_tensor(
+            w_grouped[:],
+            turned_w[:].rearrange("s t q -> s q t"),
+            size_cols[:].unsqueeze(1).to_broadcast([P, Q, PACK]),
+            ALU.mult,
+        )
+        w_codes, w_plane = quantize("w", w_grouped[:].rearrange("p q j -> p (q j)"), Q)
+
+        early = sb.tile([P, (BLOCKS - 1) * P], F32, name="early")
+        late = sb.tile([P, P], F32, name="late")
+        for b in range(BLOCKS):
+            listed_v = sb.tile([P, I], BF16, name="listed_v%d" % b, align_bytes=64)
+            nc.vector.tensor_copy(listed_v[:], pools[b][:].indirect(offsets[:]))
+            pairs = listed_v[:].bitcast(F32)
+            turned_v = ps.tile([P, 2, P], F32, name="turned_v%d" % (b % 2))
+            for u in range(2):
+                nc.tensor.transpose(turned_v[:, u, :], pairs[:, u : I // 2 : 2], ident[:])
+            v_grouped = sb.tile([P, P * PACK], BF16, name="v_grouped%d" % b, align_bytes=64)
+            nc.scalar.copy(
+                out=v_grouped[:].bitcast(F32).rearrange("p (e u) -> p e u", u=2),
+                in_=turned_v[:].rearrange("p u e -> p e u"),
+            )
+            v_codes, v_plane = quantize("v%d" % b, v_grouped[:], P)
+            sums = ps.tile([Q, P], F32, name="sums%d" % b)
+            nc.tensor.matmul_mx(
+                out=sums[:],
+                lhsT=w_codes[:].bitcast(FP8X4),
+                lhsT_scale=w_plane[:],
+                rhs=v_codes[:].bitcast(FP8X4),
+                rhs_scale=v_plane[:],
+                start=True,
+                stop=True,
+            )
+            if b < BLOCKS - 1:
+                nc.scalar.copy(out=early[:, b * P : (b + 1) * P], in_=sums[:])
+            else:
+                nc.scalar.copy(out=late[:], in_=sums[:])
+        nc.sync.dma_start(out[:, : (BLOCKS - 1) * P], early[:])
+        nc.sync.dma_start(out[:, (BLOCKS - 1) * P :], late[:])

@@ -18,7 +18,6 @@ ALU = mybir.AluOpType
 
 P = 128
 PACK = 4
-BLOCKS = E // P
 
 
 def tile_attend_signedread_kernel(tc, query, keys_words, keys_scales, steep, base0, size, vals, offs, out):
@@ -27,26 +26,65 @@ def tile_attend_signedread_kernel(tc, query, keys_words, keys_scales, steep, bas
         sb = ctx.enter_context(tc.tile_pool(name="sb", bufs=1))
         ps = ctx.enter_context(tc.psum_pool(name="ps", bufs=1))
 
+        def region(r, shape, dtype, name):
+            return sb.tile(shape, dtype, name=name, tag="region%d" % r, align_bytes=64)
+
+        def load_values(b):
+            pool_b = region(b, [P, T], F32, "val_pool%d" % b)
+            nc.sync.dma_start(pool_b[:], vals[b * P : (b + 1) * P, :])
+            return pool_b
+
+        def gather_values(b, pool_b):
+            listed_v = sb.tile([P, I], BF16, name="listed_v%d" % b, align_bytes=64)
+            nc.vector.tensor_copy(listed_v[:], pool_b[:].indirect(offsets[:]))
+            return listed_v
+
+        def turn(rows, bank, grouped):
+            pairs = rows.bitcast(F32)
+            turned = ps.tile([P, 2, P], F32, name=bank)
+            for u in range(2):
+                nc.tensor.transpose(turned[:, u, :], pairs[:, u : I // 2 : 2], ident[:])
+            nc.scalar.copy(
+                out=grouped.bitcast(F32).rearrange("p (e u) -> p e u", u=2),
+                in_=turned[:].rearrange("p u e -> p e u"),
+            )
+
+        def quantize(name, grouped, codes):
+            plane = sb.tile(list(codes.shape), U8, name=name + "_plane", align_bytes=64)
+            nc.vector.quantize_mx(out=codes[:].bitcast(FP8X4), scales=plane[:], in_=grouped)
+            return plane
+
+        def product(sums, lhs_codes, lhs_plane, rhs_codes, rhs_plane):
+            nc.tensor.matmul_mx(
+                out=sums,
+                lhsT=lhs_codes.bitcast(FP8X4),
+                lhsT_scale=lhs_plane,
+                rhs=rhs_codes.bitcast(FP8X4),
+                rhs_scale=rhs_plane,
+                start=True,
+                stop=True,
+            )
+
+        def store(name, sums, first, width):
+            staged = sb.tile([Q, width], F32, name=name)
+            nc.scalar.copy(out=staged[:], in_=sums[:])
+            nc.sync.dma_start(out[:, first : first + width], staged[:])
+
         offsets = sb.tile([P, I // 16], U16, name="offsets")
         nc.sync.dma_start(offsets[:], offs)
 
-        key_bytes = sb.tile([P, T], U8, name="key_bytes", align_bytes=64)
+        key_bytes = region(2, [P, T], U8, "key_bytes")
         nc.vector.memset(key_bytes[:].bitcast(I32), 0)
         for quad in range(4):
             nc.scalar.dma_start(
                 key_bytes[32 * quad : 32 * quad + 4, :].bitcast(I32),
                 keys_scales[0, 4 * quad : 4 * quad + 4, :].bitcast(I32),
             )
-
-        q_raw = sb.tile([P, PACK, Q], F32, name="q_raw")
+        q_raw = region(1, [P, PACK, Q], F32, "q_raw")
         nc.sync.dma_start(q_raw[:], query.rearrange("(p j) q -> p j q", j=PACK))
-        key_words = sb.tile([P, T], U32, name="key_words", align_bytes=64)
+        key_words = region(3, [P, T], U32, "key_words")
         nc.sync.dma_start(key_words[:].bitcast(I32), keys_words[0].rearrange("p n t -> p (n t)").bitcast(I32))
-        pools = []
-        for b in range(BLOCKS):
-            pool_b = sb.tile([P, T], F32, name="val_pool%d" % b, align_bytes=64)
-            nc.sync.dma_start(pool_b[:], vals[b * P : (b + 1) * P, :])
-            pools.append(pool_b)
+        pool0 = load_values(0)
 
         steep_col = sb.tile([P, 1], F32, name="steep_col")
         nc.gpsimd.dma_start(steep_col[:], steep)
@@ -57,83 +95,77 @@ def tile_attend_signedread_kernel(tc, query, keys_words, keys_scales, steep, bas
         ident = sb.tile([P, P], F32, name="ident")
         make_identity(nc, ident[:])
 
-        def quantize(name, grouped, width):
-            codes = sb.tile([P, width], U32, name=name + "_codes", align_bytes=64)
-            plane = sb.tile([P, width], U8, name=name + "_plane", align_bytes=64)
-            nc.vector.quantize_mx(out=codes[:].bitcast(FP8X4), scales=plane[:], in_=grouped)
-            return codes, plane
-
         q_grouped = sb.tile([P, Q, PACK], BF16, name="q_grouped", align_bytes=64)
-        nc.vector.tensor_copy(out=q_grouped[:], in_=q_raw[:].rearrange("p j q -> p q j"))
+        nc.scalar.copy(out=q_grouped[:], in_=q_raw[:].rearrange("p j q -> p q j"))
+        pool1 = load_values(1)
         listed_bytes = sb.tile([P, I], U8, name="listed_bytes", align_bytes=64)
         nc.vector.tensor_copy(listed_bytes[:], key_bytes[:].indirect(offsets[:]))
-        q_codes, q_plane = quantize("q", q_grouped[:].rearrange("p q j -> p (q j)"), Q)
+        pool2 = load_values(2)
+        q_codes = sb.tile([P, Q], U32, name="q_codes", align_bytes=64)
+        q_plane = quantize("q", q_grouped[:].rearrange("p q j -> p (q j)"), q_codes)
         listed_words = sb.tile([P, I], U32, name="listed_words", align_bytes=64)
         nc.vector.tensor_copy(listed_words[:], key_words[:].indirect(offsets[:]))
+        pool3 = load_values(3)
         scores = ps.tile([P, I], F32, name="scores")
-        nc.tensor.matmul_mx(
-            out=scores[:],
-            lhsT=q_codes[:].bitcast(FP8X4),
-            lhsT_scale=q_plane[:],
-            rhs=listed_words[:].bitcast(FP8X4),
-            rhs_scale=listed_bytes[:],
-            start=True,
-            stop=True,
-        )
+        product(scores[:], q_codes[:], q_plane[:], listed_words[:], listed_bytes[:])
 
-        tanhs = sb.tile([P, PACK, P], F32, name="tanhs")
-        nc.scalar.activation(
-            out=tanhs[:], in_=scores[:].rearrange("q (s t) -> q t s", t=PACK), func=ACT.Tanh, scale=steep_col[:]
-        )
-        magnitudes = sb.tile([P, PACK, P], F32, name="magnitudes")
-        row_sum = sb.tile([P, 1], F32, name="row_sum")
+        size_rows = ps.tile([Q, PACK, P], F32, name="size_rows")
+        for t in range(PACK):
+            nc.tensor.transpose(size_rows[:, t, :], size_cols[:, t : t + 1].to_broadcast([P, Q]), ident[:])
+        tanhs = sb.tile([Q, I], F32, name="tanhs")
+        nc.scalar.activation(out=tanhs[:], in_=scores[:], func=ACT.Tanh, scale=steep_col[:])
+        magnitudes = sb.tile([Q, I], F32, name="magnitudes")
+        row_sum = sb.tile([Q, 1], F32, name="row_sum")
         nc.scalar.activation(
             out=magnitudes[:], in_=tanhs[:], func=ACT.Abs, scale=-1.0, bias=base_col[:], accum_out=row_sum[:]
         )
-        row_inv = sb.tile([P, 1], F32, name="row_inv")
-        nc.vector.reciprocal(row_inv[:], row_sum[:])
-        normed = sb.tile([P, PACK, P], F32, name="normed")
-        nc.vector.tensor_scalar(normed[:], tanhs[:], base_col[:], row_inv[:], ALU.subtract, ALU.mult)
-        turned_w = ps.tile([P, PACK, Q], F32, name="turned_w")
-        for t in range(PACK):
-            nc.tensor.transpose(turned_w[:, t, :], normed[:, t, :], ident[:])
-        w_grouped = sb.tile([P, Q, PACK], BF16, name="w_grouped", align_bytes=64)
-        nc.vector.tensor_tensor(
-            w_grouped[:],
-            turned_w[:].rearrange("s t q -> s q t"),
-            size_cols[:].unsqueeze(1).to_broadcast([P, Q, PACK]),
+
+        listed0 = gather_values(0, pool0)
+        sized_and_inv = region(0, [Q, I + 1], F32, "sized_and_inv")
+        sized = sized_and_inv[:, :I]
+        row_inv = sized_and_inv[:, I : I + 1]
+        nc.vector.scalar_tensor_tensor(
+            sized.rearrange("q (s t) -> q s t", t=PACK),
+            tanhs[:].rearrange("q (s t) -> q s t", t=PACK),
+            base_col[:],
+            size_rows[:].rearrange("q t s -> q s t"),
+            ALU.subtract,
             ALU.mult,
         )
-        w_codes, w_plane = quantize("w", w_grouped[:].rearrange("p q j -> p (q j)"), Q)
+        nc.vector.reciprocal(row_inv, row_sum[:])
+        wv_grouped = sb.tile([P, 2 * I], BF16, name="wv_grouped", align_bytes=64)
+        turn(listed0[:], "turned_a", wv_grouped[:, I:])
+        weights = sb.tile([Q, I], BF16, name="weights", align_bytes=64)
+        nc.scalar.activation(out=weights[:], in_=sized, func=ACT.Copy, scale=row_inv)
+        turn(weights[:], "turned_w", wv_grouped[:, :I])
 
-        early = sb.tile([P, (BLOCKS - 1) * P], F32, name="early")
-        late = sb.tile([P, P], F32, name="late")
-        for b in range(BLOCKS):
-            listed_v = sb.tile([P, I], BF16, name="listed_v%d" % b, align_bytes=64)
-            nc.vector.tensor_copy(listed_v[:], pools[b][:].indirect(offsets[:]))
-            pairs = listed_v[:].bitcast(F32)
-            turned_v = ps.tile([P, 2, P], F32, name="turned_v%d" % (b % 2))
-            for u in range(2):
-                nc.tensor.transpose(turned_v[:, u, :], pairs[:, u : I // 2 : 2], ident[:])
-            v_grouped = sb.tile([P, P * PACK], BF16, name="v_grouped%d" % b, align_bytes=64)
-            nc.scalar.copy(
-                out=v_grouped[:].bitcast(F32).rearrange("p (e u) -> p e u", u=2),
-                in_=turned_v[:].rearrange("p u e -> p e u"),
-            )
-            v_codes, v_plane = quantize("v%d" % b, v_grouped[:], P)
-            sums = ps.tile([Q, P], F32, name="sums%d" % b)
-            nc.tensor.matmul_mx(
-                out=sums[:],
-                lhsT=w_codes[:].bitcast(FP8X4),
-                lhsT_scale=w_plane[:],
-                rhs=v_codes[:].bitcast(FP8X4),
-                rhs_scale=v_plane[:],
-                start=True,
-                stop=True,
-            )
-            if b < BLOCKS - 1:
-                nc.scalar.copy(out=early[:, b * P : (b + 1) * P], in_=sums[:])
-            else:
-                nc.scalar.copy(out=late[:], in_=sums[:])
-        nc.sync.dma_start(out[:, : (BLOCKS - 1) * P], early[:])
-        nc.sync.dma_start(out[:, (BLOCKS - 1) * P :], late[:])
+        listed1 = gather_values(1, pool1)
+        wv_codes = region(1, [P, 2 * P], U32, "wv_codes")
+        wv_plane = quantize("wv", wv_grouped[:], wv_codes)
+        w_codes, w_plane = wv_codes[:, :P], wv_plane[:, :P]
+        sums01 = ps.tile([Q, 2 * P], F32, name="sums01")
+        product(sums01[:, :P], w_codes, w_plane, wv_codes[:, P:], wv_plane[:, P:])
+        grouped1 = sb.tile([P, I], BF16, name="grouped1", align_bytes=64)
+        turn(listed1[:], "turned_b", grouped1[:])
+
+        listed2 = gather_values(2, pool2)
+        codes1 = region(2, [P, P], U32, "codes1")
+        plane1 = quantize("v1", grouped1[:], codes1)
+        product(sums01[:, P:], w_codes, w_plane, codes1[:], plane1[:])
+        grouped2 = sb.tile([P, I], BF16, name="grouped2", align_bytes=64)
+        turn(listed2[:], "turned_a", grouped2[:])
+        store("staged01", sums01, 0, 2 * P)
+
+        listed3 = gather_values(3, pool3)
+        codes2 = region(3, [P, P], U32, "codes2")
+        plane2 = quantize("v2", grouped2[:], codes2)
+        grouped3 = sb.tile([P, I], BF16, name="grouped3", align_bytes=64)
+        turn(listed3[:], "turned_b", grouped3[:])
+        sums2 = ps.tile([Q, P], F32, name="sums2")
+        product(sums2[:], w_codes, w_plane, codes2[:], plane2[:])
+        store("staged2", sums2, 2 * P, P)
+        codes3 = sb.tile([P, P], U32, name="codes3", align_bytes=64)
+        plane3 = quantize("v3", grouped3[:], codes3)
+        sums3 = ps.tile([Q, P], F32, name="sums3")
+        product(sums3[:], w_codes, w_plane, codes3[:], plane3[:])
+        store("staged3", sums3, 3 * P, P)

@@ -73,39 +73,37 @@ def tile_attend_signedread_kernel(tc, query, keys_words, keys_scales, steep, bas
         offsets = sb.tile([P, I // 16], U16, name="offsets")
         nc.sync.dma_start(offsets[:], offs)
 
-        key_bytes = region(2, [P, T], U8, "key_bytes")
-        nc.vector.memset(key_bytes[:].bitcast(I32), 0)
+        key_bytes = sb.tile([P, T], U8, name="key_bytes", align_bytes=64)
+        nc.gpsimd.memset(key_bytes[:].bitcast(I32), 0)
+        ident = sb.tile([P, P], F32, name="ident")
+        make_identity(nc, ident[:])
+        size_cols = sb.tile([P, PACK], F32, name="size_cols")
+        nc.sync.dma_start(size_cols[:], size.rearrange("o (p t) -> (o p) t", t=PACK))
+        q_raw = sb.tile([P, PACK, Q], F32, name="q_raw")
+        nc.sync.dma_start(q_raw[:], query.rearrange("(p j) q -> p j q", j=PACK))
         for quad in range(4):
-            nc.scalar.dma_start(
+            nc.sync.dma_start(
                 key_bytes[32 * quad : 32 * quad + 4, :].bitcast(I32),
                 keys_scales[0, 4 * quad : 4 * quad + 4, :].bitcast(I32),
             )
-        q_raw = region(1, [P, PACK, Q], F32, "q_raw")
-        nc.sync.dma_start(q_raw[:], query.rearrange("(p j) q -> p j q", j=PACK))
-        key_words = region(3, [P, T], U32, "key_words")
+        key_words = sb.tile([P, T], U32, name="key_words", align_bytes=64)
         nc.sync.dma_start(key_words[:].bitcast(I32), keys_words[0].rearrange("p n t -> p (n t)").bitcast(I32))
         pool0 = load_values(0)
-
         steep_col = sb.tile([P, 1], F32, name="steep_col")
-        nc.gpsimd.dma_start(steep_col[:], steep)
+        nc.sync.dma_start(steep_col[:], steep)
         base_col = sb.tile([P, 1], F32, name="base_col")
-        nc.gpsimd.dma_start(base_col[:], base0)
-        size_cols = sb.tile([P, PACK], F32, name="size_cols")
-        nc.gpsimd.dma_start(size_cols[:], size.rearrange("o (p t) -> (o p) t", t=PACK))
-        ident = sb.tile([P, P], F32, name="ident")
-        make_identity(nc, ident[:])
+        nc.sync.dma_start(base_col[:], base0)
+        pool1, pool2, pool3 = [load_values(b) for b in range(1, 4)]
+
 
         q_grouped = sb.tile([P, Q, PACK], BF16, name="q_grouped", align_bytes=64)
         nc.scalar.copy(out=q_grouped[:], in_=q_raw[:].rearrange("p j q -> p q j"))
-        pool1 = load_values(1)
-        listed_bytes = sb.tile([P, I], U8, name="listed_bytes", align_bytes=64)
-        nc.vector.tensor_copy(listed_bytes[:], key_bytes[:].indirect(offsets[:]))
-        pool2 = load_values(2)
         q_codes = sb.tile([P, Q], U32, name="q_codes", align_bytes=64)
         q_plane = quantize("q", q_grouped[:].rearrange("p q j -> p (q j)"), q_codes)
+        listed_bytes = sb.tile([P, I], U8, name="listed_bytes", align_bytes=64)
+        nc.vector.tensor_copy(listed_bytes[:], key_bytes[:].indirect(offsets[:]))
         listed_words = sb.tile([P, I], U32, name="listed_words", align_bytes=64)
         nc.vector.tensor_copy(listed_words[:], key_words[:].indirect(offsets[:]))
-        pool3 = load_values(3)
         scores = ps.tile([P, I], F32, name="scores")
         product(scores[:], q_codes[:], q_plane[:], listed_words[:], listed_bytes[:])
 
@@ -133,25 +131,25 @@ def tile_attend_signedread_kernel(tc, query, keys_words, keys_scales, steep, bas
             ALU.mult,
         )
         nc.vector.reciprocal(row_inv, row_sum[:])
-        wv_grouped = sb.tile([P, 2 * I], BF16, name="wv_grouped", align_bytes=64)
-        turn(listed0[:], "turned_a", wv_grouped[:, I:])
+        grouped0 = sb.tile([P, I], BF16, name="grouped0", align_bytes=64)
+        turn(listed0[:], "turned_a", grouped0[:])
         weights = sb.tile([Q, I], BF16, name="weights", align_bytes=64)
         nc.scalar.activation(out=weights[:], in_=sized, func=ACT.Copy, scale=row_inv)
+        wv_grouped = sb.tile([P, 2 * I], BF16, name="wv_grouped", align_bytes=64)
         turn(weights[:], "turned_w", wv_grouped[:, :I])
 
         listed1 = gather_values(1, pool1)
-        wv_codes = region(1, [P, 2 * P], U32, "wv_codes")
+        codes0 = region(1, [P, P], U32, "codes0")
+        plane0 = quantize("v0", grouped0[:], codes0)
+        turn(listed1[:], "turned_b", wv_grouped[:, I:])
+
+        listed2 = gather_values(2, pool2)
+        wv_codes = region(2, [P, 2 * P], U32, "wv_codes")
         wv_plane = quantize("wv", wv_grouped[:], wv_codes)
         w_codes, w_plane = wv_codes[:, :P], wv_plane[:, :P]
         sums01 = ps.tile([Q, 2 * P], F32, name="sums01")
-        product(sums01[:, :P], w_codes, w_plane, wv_codes[:, P:], wv_plane[:, P:])
-        grouped1 = sb.tile([P, I], BF16, name="grouped1", align_bytes=64)
-        turn(listed1[:], "turned_b", grouped1[:])
-
-        listed2 = gather_values(2, pool2)
-        codes1 = region(2, [P, P], U32, "codes1")
-        plane1 = quantize("v1", grouped1[:], codes1)
-        product(sums01[:, P:], w_codes, w_plane, codes1[:], plane1[:])
+        product(sums01[:, :P], w_codes, w_plane, codes0[:], plane0[:])
+        product(sums01[:, P:], w_codes, w_plane, wv_codes[:, P:], wv_plane[:, P:])
         grouped2 = sb.tile([P, I], BF16, name="grouped2", align_bytes=64)
         turn(listed2[:], "turned_a", grouped2[:])
         store("staged01", sums01, 0, 2 * P)

@@ -18,6 +18,8 @@ ALU = mybir.AluOpType
 
 P = 128
 PACK = 4
+QUADRANT = 32
+SCALE_ROWS = D // 32
 
 
 def tile_attend_signedread_kernel(tc, query, keys_words, keys_scales, steep, base0, size, vals, offs, out):
@@ -26,8 +28,8 @@ def tile_attend_signedread_kernel(tc, query, keys_words, keys_scales, steep, bas
         sb = ctx.enter_context(tc.tile_pool(name="sb", bufs=1))
         ps = ctx.enter_context(tc.psum_pool(name="ps", bufs=1))
 
-        def region(r, shape, dtype, name):
-            return sb.tile(shape, dtype, name=name, tag="region%d" % r, align_bytes=64)
+        def region(b, shape, dtype, name):
+            return sb.tile(shape, dtype, name=name, tag="region%d" % b, align_bytes=64)
 
         def load_values(b):
             pool_b = region(b, [P, T], F32, "val_pool%d" % b)
@@ -50,17 +52,17 @@ def tile_attend_signedread_kernel(tc, query, keys_words, keys_scales, steep, bas
             )
 
         def quantize(name, grouped, codes):
-            plane = sb.tile(list(codes.shape), U8, name=name + "_plane", align_bytes=64)
-            nc.vector.quantize_mx(out=codes[:].bitcast(FP8X4), scales=plane[:], in_=grouped)
-            return plane
+            scale_bytes = sb.tile(list(codes.shape), U8, name=name + "_plane", align_bytes=64)
+            nc.vector.quantize_mx(out=codes[:].bitcast(FP8X4), scales=scale_bytes[:], in_=grouped)
+            return scale_bytes
 
-        def product(sums, lhs_codes, lhs_plane, rhs_codes, rhs_plane):
+        def product(sums, lhs_codes, lhs_scales, rhs_codes, rhs_scales):
             nc.tensor.matmul_mx(
                 out=sums,
                 lhsT=lhs_codes.bitcast(FP8X4),
-                lhsT_scale=lhs_plane,
+                lhsT_scale=lhs_scales,
                 rhs=rhs_codes.bitcast(FP8X4),
-                rhs_scale=rhs_plane,
+                rhs_scale=rhs_scales,
                 start=True,
                 stop=True,
             )
@@ -77,17 +79,16 @@ def tile_attend_signedread_kernel(tc, query, keys_words, keys_scales, steep, bas
         nc.gpsimd.memset(key_bytes[:].bitcast(I32), 0)
         ident = sb.tile([P, P], F32, name="ident")
         make_identity(nc, ident[:])
-        size_cols = sb.tile([P, PACK], F32, name="size_cols")
-        nc.sync.dma_start(size_cols[:], size.rearrange("o (p t) -> (o p) t", t=PACK))
-        q_raw = sb.tile([P, PACK, Q], F32, name="q_raw")
-        nc.sync.dma_start(q_raw[:], query.rearrange("(p j) q -> p j q", j=PACK))
-        for quad in range(4):
-            nc.sync.dma_start(
-                key_bytes[32 * quad : 32 * quad + 4, :].bitcast(I32),
-                keys_scales[0, 4 * quad : 4 * quad + 4, :].bitcast(I32),
-            )
         key_words = sb.tile([P, T], U32, name="key_words", align_bytes=64)
         nc.sync.dma_start(key_words[:].bitcast(I32), keys_words[0].rearrange("p n t -> p (n t)").bitcast(I32))
+        q_raw = sb.tile([P, PACK, Q], F32, name="q_raw")
+        nc.sync.dma_start(q_raw[:], query.rearrange("(p j) q -> p j q", j=PACK))
+        size_cols = sb.tile([P, PACK], F32, name="size_cols")
+        nc.sync.dma_start(size_cols[:], size.rearrange("o (p t) -> (o p) t", t=PACK))
+        for r in range(4):
+            nc.sync.dma_start(
+                key_bytes[r:P:QUADRANT, :].bitcast(I32), keys_scales[0, r:SCALE_ROWS:4, :].bitcast(I32)
+            )
         pool0 = load_values(0)
         steep_col = sb.tile([P, 1], F32, name="steep_col")
         nc.sync.dma_start(steep_col[:], steep)
@@ -95,17 +96,16 @@ def tile_attend_signedread_kernel(tc, query, keys_words, keys_scales, steep, bas
         nc.sync.dma_start(base_col[:], base0)
         pool1, pool2, pool3 = [load_values(b) for b in range(1, 4)]
 
-
-        q_grouped = sb.tile([P, Q, PACK], BF16, name="q_grouped", align_bytes=64)
-        nc.scalar.copy(out=q_grouped[:], in_=q_raw[:].rearrange("p j q -> p q j"))
-        q_codes = sb.tile([P, Q], U32, name="q_codes", align_bytes=64)
-        q_plane = quantize("q", q_grouped[:].rearrange("p q j -> p (q j)"), q_codes)
-        listed_bytes = sb.tile([P, I], U8, name="listed_bytes", align_bytes=64)
-        nc.vector.tensor_copy(listed_bytes[:], key_bytes[:].indirect(offsets[:]))
         listed_words = sb.tile([P, I], U32, name="listed_words", align_bytes=64)
         nc.vector.tensor_copy(listed_words[:], key_words[:].indirect(offsets[:]))
+        q_grouped = sb.tile([P, Q, PACK], BF16, name="q_grouped", align_bytes=64)
+        nc.scalar.copy(out=q_grouped[:], in_=q_raw[:].rearrange("p j q -> p q j"))
+        listed_bytes = sb.tile([P, I], U8, name="listed_bytes", align_bytes=64)
+        nc.vector.tensor_copy(listed_bytes[:], key_bytes[:].indirect(offsets[:]))
+        q_codes = sb.tile([P, Q], U32, name="q_codes", align_bytes=64)
+        q_scales = quantize("q", q_grouped[:].rearrange("p q j -> p (q j)"), q_codes)
         scores = ps.tile([P, I], F32, name="scores")
-        product(scores[:], q_codes[:], q_plane[:], listed_words[:], listed_bytes[:])
+        product(scores[:], q_codes[:], q_scales[:], listed_words[:], listed_bytes[:])
 
         size_rows = ps.tile([Q, PACK, P], F32, name="size_rows")
         for t in range(PACK):
@@ -131,39 +131,34 @@ def tile_attend_signedread_kernel(tc, query, keys_words, keys_scales, steep, bas
             ALU.mult,
         )
         nc.vector.reciprocal(row_inv, row_sum[:])
-        grouped0 = sb.tile([P, I], BF16, name="grouped0", align_bytes=64)
-        turn(listed0[:], "turned_a", grouped0[:])
+        grouped01 = sb.tile([P, 2 * I], BF16, name="grouped01", align_bytes=64)
+        turn(listed0[:], "turned_a", grouped01[:, :I])
         weights = sb.tile([Q, I], BF16, name="weights", align_bytes=64)
         nc.scalar.activation(out=weights[:], in_=sized, func=ACT.Copy, scale=row_inv)
-        wv_grouped = sb.tile([P, 2 * I], BF16, name="wv_grouped", align_bytes=64)
-        turn(weights[:], "turned_w", wv_grouped[:, :I])
 
         listed1 = gather_values(1, pool1)
-        codes0 = region(1, [P, P], U32, "codes0")
-        plane0 = quantize("v0", grouped0[:], codes0)
-        turn(listed1[:], "turned_b", wv_grouped[:, I:])
+        turn(listed1[:], "turned_b", grouped01[:, I:])
+        grouped_w2 = sb.tile([P, 2 * I], BF16, name="grouped_w2", align_bytes=64)
+        turn(weights[:], "turned_w", grouped_w2[:, :I])
 
         listed2 = gather_values(2, pool2)
-        wv_codes = region(2, [P, 2 * P], U32, "wv_codes")
-        wv_plane = quantize("wv", wv_grouped[:], wv_codes)
-        w_codes, w_plane = wv_codes[:, :P], wv_plane[:, :P]
-        sums01 = ps.tile([Q, 2 * P], F32, name="sums01")
-        product(sums01[:, :P], w_codes, w_plane, codes0[:], plane0[:])
-        product(sums01[:, P:], w_codes, w_plane, wv_codes[:, P:], wv_plane[:, P:])
-        grouped2 = sb.tile([P, I], BF16, name="grouped2", align_bytes=64)
-        turn(listed2[:], "turned_a", grouped2[:])
-        store("staged01", sums01, 0, 2 * P)
+        codes01 = region(2, [P, 2 * P], U32, "codes01")
+        scales01 = quantize("v01", grouped01[:], codes01)
+        turn(listed2[:], "turned_a", grouped_w2[:, I:])
 
         listed3 = gather_values(3, pool3)
-        codes2 = region(3, [P, P], U32, "codes2")
-        plane2 = quantize("v2", grouped2[:], codes2)
+        codes_w2 = region(3, [P, 2 * P], U32, "codes_w2")
+        scales_w2 = quantize("w2", grouped_w2[:], codes_w2)
+        w_codes, w_scales = codes_w2[:, :P], scales_w2[:, :P]
         grouped3 = sb.tile([P, I], BF16, name="grouped3", align_bytes=64)
         turn(listed3[:], "turned_b", grouped3[:])
-        sums2 = ps.tile([Q, P], F32, name="sums2")
-        product(sums2[:], w_codes, w_plane, codes2[:], plane2[:])
-        store("staged2", sums2, 2 * P, P)
+
+        sums012 = ps.tile([Q, 3 * P], F32, name="sums012")
+        product(sums012[:, : 2 * P], w_codes, w_scales, codes01[:], scales01[:])
+        product(sums012[:, 2 * P :], w_codes, w_scales, codes_w2[:, P:], scales_w2[:, P:])
+        store("staged012", sums012, 0, 3 * P)
         codes3 = sb.tile([P, P], U32, name="codes3", align_bytes=64)
-        plane3 = quantize("v3", grouped3[:], codes3)
+        scales3 = quantize("v3", grouped3[:], codes3)
         sums3 = ps.tile([Q, P], F32, name="sums3")
-        product(sums3[:], w_codes, w_plane, codes3[:], plane3[:])
+        product(sums3[:], w_codes, w_scales, codes3[:], scales3[:])
         store("staged3", sums3, 3 * P, P)

from contextlib import ExitStack

import concourse.mybir as mybir
from concourse.masks import make_identity

D, T, I, Q, E = 512, 2048, 512, 128, 512
FLOPS = 2 * Q * D * I + 2 * Q * I * E

F32 = mybir.dt.float32
BF16 = mybir.dt.bfloat16
I32 = mybir.dt.int32
U32 = mybir.dt.uint32
U16 = mybir.dt.uint16
U8 = mybir.dt.uint8
FP8X4 = mybir.dt.float8_e4m3fn_x4
ACT = mybir.ActivationFunctionType
ALU = mybir.AluOpType

P = 128
PACK = 4
QUADRANT = 32
SCALE_ROWS = D // 32


def tile_attend_signedread_kernel(tc, query, keys_words, keys_scales, steep, base0, size, vals, offs, out):
    nc = tc.nc
    with ExitStack() as ctx:
        sb = ctx.enter_context(tc.tile_pool(name="sb", bufs=1))
        ps = ctx.enter_context(tc.psum_pool(name="ps", bufs=1))

        def region(b, shape, dtype, name):
            return sb.tile(shape, dtype, name=name, tag="region%d" % b, align_bytes=64)

        def load_values(b):
            pool_b = region(b, [P, T], F32, "val_pool%d" % b)
            nc.sync.dma_start(pool_b[:], vals[b * P : (b + 1) * P, :])
            return pool_b

        def gather_values(b, pool_b):
            listed_v = sb.tile([P, I], BF16, name="listed_v%d" % b, align_bytes=64)
            nc.vector.tensor_copy(listed_v[:], pool_b[:].indirect(offsets[:]))
            return listed_v

        def turn(rows, bank, grouped):
            pairs = rows.bitcast(F32)
            turned = ps.tile([P, 2, P], F32, name=bank)
            for u in range(2):
                nc.tensor.transpose(turned[:, u, :], pairs[:, u : I // 2 : 2], ident[:])
            nc.scalar.copy(
                out=grouped.bitcast(F32).rearrange("p (e u) -> p e u", u=2),
                in_=turned[:].rearrange("p u e -> p e u"),
            )

        def quantize(name, grouped, codes):
            scale_bytes = sb.tile(list(codes.shape), U8, name=name + "_plane", align_bytes=64)
            nc.vector.quantize_mx(out=codes[:].bitcast(FP8X4), scales=scale_bytes[:], in_=grouped)
            return scale_bytes

        def product(sums, lhs_codes, lhs_scales, rhs_codes, rhs_scales):
            nc.tensor.matmul_mx(
                out=sums,
                lhsT=lhs_codes.bitcast(FP8X4),
                lhsT_scale=lhs_scales,
                rhs=rhs_codes.bitcast(FP8X4),
                rhs_scale=rhs_scales,
                start=True,
                stop=True,
            )

        def store(name, sums, first, width):
            staged = sb.tile([Q, width], F32, name=name)
            nc.scalar.copy(out=staged[:], in_=sums[:])
            nc.sync.dma_start(out[:, first : first + width], staged[:])

        offsets = sb.tile([P, I // 16], U16, name="offsets")
        nc.sync.dma_start(offsets[:], offs)

        key_bytes = sb.tile([P, T], U8, name="key_bytes", align_bytes=64)
        nc.gpsimd.memset(key_bytes[:].bitcast(I32), 0)
        ident = sb.tile([P, P], F32, name="ident")
        make_identity(nc, ident[:])
        key_words = sb.tile([P, T], U32, name="key_words", align_bytes=64)
        nc.sync.dma_start(key_words[:].bitcast(I32), keys_words[0].rearrange("p n t -> p (n t)").bitcast(I32))
        q_raw = sb.tile([P, PACK, Q], F32, name="q_raw")
        nc.sync.dma_start(q_raw[:], query.rearrange("(p j) q -> p j q", j=PACK))
        size_cols = sb.tile([P, PACK], F32, name="size_cols")
        nc.sync.dma_start(size_cols[:], size.rearrange("o (p t) -> (o p) t", t=PACK))
        for r in range(4):
            nc.sync.dma_start(
                key_bytes[r:P:QUADRANT, :].bitcast(I32), keys_scales[0, r:SCALE_ROWS:4, :].bitcast(I32)
            )
        pool0 = load_values(0)
        steep_col = sb.tile([P, 1], F32, name="steep_col")
        nc.sync.dma_start(steep_col[:], steep)
        base_col = sb.tile([P, 1], F32, name="base_col")
        nc.sync.dma_start(base_col[:], base0)
        pool1, pool2, pool3 = [load_values(b) for b in range(1, 4)]

        listed_words = sb.tile([P, I], U32, name="listed_words", align_bytes=64)
        nc.vector.tensor_copy(listed_words[:], key_words[:].indirect(offsets[:]))
        q_grouped = sb.tile([P, Q, PACK], BF16, name="q_grouped", align_bytes=64)
        nc.scalar.copy(out=q_grouped[:], in_=q_raw[:].rearrange("p j q -> p q j"))
        listed_bytes = sb.tile([P, I], U8, name="listed_bytes", align_bytes=64)
        nc.vector.tensor_copy(listed_bytes[:], key_bytes[:].indirect(offsets[:]))
        q_codes = sb.tile([P, Q], U32, name="q_codes", align_bytes=64)
        q_scales = quantize("q", q_grouped[:].rearrange("p q j -> p (q j)"), q_codes)
        scores = ps.tile([P, I], F32, name="scores")
        product(scores[:], q_codes[:], q_scales[:], listed_words[:], listed_bytes[:])

        size_rows = ps.tile([Q, PACK, P], F32, name="size_rows")
        for t in range(PACK):
            nc.tensor.transpose(size_rows[:, t, :], size_cols[:, t : t + 1].to_broadcast([P, Q]), ident[:])
        tanhs = sb.tile([Q, I], F32, name="tanhs")
        nc.scalar.activation(out=tanhs[:], in_=scores[:], func=ACT.Tanh, scale=steep_col[:])
        magnitudes = sb.tile([Q, I], F32, name="magnitudes")
        row_sum = sb.tile([Q, 1], F32, name="row_sum")
        nc.scalar.activation(
            out=magnitudes[:], in_=tanhs[:], func=ACT.Abs, scale=-1.0, bias=base_col[:], accum_out=row_sum[:]
        )

        listed0 = gather_values(0, pool0)
        sized_and_inv = region(0, [Q, I + 1], F32, "sized_and_inv")
        sized = sized_and_inv[:, :I]
        row_inv = sized_and_inv[:, I : I + 1]
        nc.vector.scalar_tensor_tensor(
            sized.rearrange("q (s t) -> q s t", t=PACK),
            tanhs[:].rearrange("q (s t) -> q s t", t=PACK),
            base_col[:],
            size_rows[:].rearrange("q t s -> q s t"),
            ALU.subtract,
            ALU.mult,
        )
        nc.vector.reciprocal(row_inv, row_sum[:])
        grouped01 = sb.tile([P, 2 * I], BF16, name="grouped01", align_bytes=64)
        turn(listed0[:], "turned_a", grouped01[:, :I])
        weights = sb.tile([Q, I], BF16, name="weights", align_bytes=64)
        nc.scalar.activation(out=weights[:], in_=sized, func=ACT.Copy, scale=row_inv)

        listed1 = gather_values(1, pool1)
        turn(listed1[:], "turned_b", grouped01[:, I:])
        grouped_w2 = sb.tile([P, 2 * I], BF16, name="grouped_w2", align_bytes=64)
        turn(weights[:], "turned_w", grouped_w2[:, :I])

        listed2 = gather_values(2, pool2)
        codes01 = region(2, [P, 2 * P], U32, "codes01")
        scales01 = quantize("v01", grouped01[:], codes01)
        turn(listed2[:], "turned_a", grouped_w2[:, I:])

        listed3 = gather_values(3, pool3)
        codes_w2 = region(3, [P, 2 * P], U32, "codes_w2")
        scales_w2 = quantize("w2", grouped_w2[:], codes_w2)
        w_codes, w_scales = codes_w2[:, :P], scales_w2[:, :P]
        grouped3 = sb.tile([P, I], BF16, name="grouped3", align_bytes=64)
        turn(listed3[:], "turned_b", grouped3[:])

        sums012 = ps.tile([Q, 3 * P], F32, name="sums012")
        product(sums012[:, : 2 * P], w_codes, w_scales, codes01[:], scales01[:])
        product(sums012[:, 2 * P :], w_codes, w_scales, codes_w2[:, P:], scales_w2[:, P:])
        store("staged012", sums012, 0, 3 * P)
        codes3 = sb.tile([P, P], U32, name="codes3", align_bytes=64)
        scales3 = quantize("v3", grouped3[:], codes3)
        sums3 = ps.tile([Q, P], F32, name="sums3")
        product(sums3[:], w_codes, w_scales, codes3[:], scales3[:])
        store("staged3", sums3, 3 * P, P)
